import numpy as np
import ml_dtypes


def mxq(x, axis, fmt="e4m3"):
    dtype, down = {"e4m3": (ml_dtypes.float8_e4m3fn, 7), "e5m2": (ml_dtypes.float8_e5m2, 14)}[fmt]
    v = np.moveaxis(np.asarray(x, np.float32).astype(ml_dtypes.bfloat16).astype(np.float64), axis, -1)
    blocks = v.reshape(v.shape[:-1] + (-1, 32))
    amax = np.abs(blocks).max(-1, keepdims=True)
    byte = np.maximum(np.where(amax > 0, np.frexp(amax)[1] - 1 + 127, 0) - down, 1)
    scale = np.exp2(byte - 127.0)
    codes = (blocks / scale).astype(np.float32).astype(dtype).astype(np.float64)
    return np.moveaxis((codes * scale).reshape(v.shape), -1, axis)


WIDE = False


def mx_kscale(k):
    if not WIDE:
        return np.ones(k)
    levels = np.array([10, -10, 5, -5, 0])
    if k % 512:
        return np.exp2(np.random.permutation(np.resize(levels, k // 32))).repeat(32)
    a = np.empty((k // 512, 16))
    for p in range(k // 512):
        a[p, :8] = np.random.permutation(np.resize(levels, 8))
        for g in range(8):
            far = levels[np.abs(levels - a[p, g]) >= 10]
            a[p, g + 8] = far[np.random.randint(len(far))]
    return np.exp2(a.ravel()).repeat(32)


def f64(x):
    return np.asarray(x).astype(np.float64)


def striped(idx):
    return np.tile(np.asarray(idx).reshape(-1, 16).T, (8, 1)).astype(np.uint16)


def unstriped(offs):
    return offs[:16].T.reshape(-1).astype(np.int64)


E2M1 = np.array([0.0, 0.5, 1.0, 1.5, 2.0, 3.0, 4.0, 6.0, -0.0, -0.5, -1.0, -1.5, -2.0, -3.0, -4.0, -6.0])


def pack_weight(w, fmt):
    k, n = w.shape
    w = f64(np.asarray(w, np.float32).astype(ml_dtypes.bfloat16)).reshape(k // 32, 32, n)
    amax = np.abs(w).max(1)
    if fmt == "e4m3":
        byte = np.frexp(amax)[1] - 1 + 127 - 7
    else:
        mant, ex = np.frexp(amax / 6.0)
        byte = np.where(mant > 0.5, ex, ex - 1) + 127
    byte = np.clip(np.where(amax > 0, byte, 1), 1, 254)
    scaled = (w * np.exp2(127.0 - byte)[:, None, :]).reshape(k, n).astype(np.float32)
    by_word = np.ascontiguousarray(scaled.reshape(k // 512, 128, 4, n).transpose(0, 1, 3, 2))
    if fmt == "e4m3":
        words = by_word.astype(ml_dtypes.float8_e4m3fn).view(np.uint8)
    else:
        c = by_word.astype(ml_dtypes.float4_e2m1fn).view(np.uint8) & 0xF
        words = (c[..., 0::2] | (c[..., 1::2] << 4)).reshape(k // 512, 128, 2 * n)
    return np.ascontiguousarray(words), np.ascontiguousarray(byte.astype(np.uint8).reshape(k // 512, 16, n))


def unpack_weight(words, scales, fmt):
    g, _, n = scales.shape
    words = np.ascontiguousarray(words).reshape(g, 128, n, -1)
    if fmt == "e4m3":
        vals = words.view(ml_dtypes.float8_e4m3fn).astype(np.float64)
    else:
        nib = np.empty((g, 128, n, 4), np.uint8)
        nib[..., 0::2] = words & 0xF
        nib[..., 1::2] = words >> 4
        vals = E2M1[nib]
    vals = vals * np.repeat(np.exp2(scales.astype(np.float64) - 127.0), 8, axis=1)[..., None]
    return vals.transpose(0, 1, 3, 2).reshape(g * 512, n)


D, K, T, U, I, E = 512, 512, 2048, 1024, 512, 256


def setup_inputs():
    n = np.random.standard_normal
    idx = np.random.permutation(T)[:I]
    idx2 = np.random.permutation(U)[:I]
    idx3 = np.random.permutation(U)[:I]
    fd = mx_kscale(D)
    fk = mx_kscale(K)
    pagesp = pack_weight(n((D, T)) / fd[:, None], "e4m3")
    wap = pack_weight(n((D, K)) * 1.0 / np.sqrt(D) * fd[:, None], "e2m1")
    notesp = pack_weight(n((D, U)) / fd[:, None], "e2m1")
    wbp = pack_weight(n((D, K)) * 1.0 / np.sqrt(D) * fd[:, None], "e4m3")
    wop = pack_weight(n((K, E)) * 1.0 / np.sqrt(K) / fk[:, None], "e2m1")
    return {
        "pages_words": pagesp[0],
        "pages_scales": pagesp[1],
        "wa_words": wap[0],
        "wa_scales": wap[1],
        "notes_words": notesp[0],
        "notes_scales": notesp[1],
        "wb_words": wbp[0],
        "wb_scales": wbp[1],
        "kf": (np.random.uniform(0.5, 2.0, (K, 1)) * fk[:, None]).astype(np.float32),
        "wo_words": wop[0],
        "wo_scales": wop[1],
        "offs": striped(idx),
        "offs2": striped(idx2),
        "offs3": striped(idx3),
    }


def reference(pages_words, pages_scales, wa_words, wa_scales, notes_words, notes_scales, wb_words, wb_scales, kf, wo_words, wo_scales, offs, offs2, offs3):
    idx = unstriped(offs)
    idx2 = unstriped(offs2)
    idx3 = unstriped(offs3)
    pagesu = unpack_weight(pages_words, pages_scales, "e4m3")
    wau = unpack_weight(wa_words, wa_scales, "e2m1")
    notesu = unpack_weight(notes_words, notes_scales, "e2m1")
    wbu = unpack_weight(wb_words, wb_scales, "e4m3")
    wou = unpack_weight(wo_words, wo_scales, "e2m1")
    pagesidxg = pagesu[:, idx]
    z = wau.T @ pagesidxg
    h1 = wbu.T @ notesu
    f1 = np.zeros((K, U))
    f1[:, idx2] = z
    c1 = h1 + f1
    w = c1[:, idx3] * f64(kf)
    wq = mxq(w, 0, "e4m3")
    y = wou.T @ wq
    return y

@@ -1,0 +1,169 @@
+from contextlib import ExitStack
+
+import concourse.mybir as mybir
+
+D, K, T, U, I, E = 512, 512, 2048, 1024, 512, 256
+FLOPS = 2 * D * K * I + 2 * D * K * U + 2 * K * E * I
+
+F32 = mybir.dt.float32
+BF16 = mybir.dt.bfloat16
+I32 = mybir.dt.int32
+U32 = mybir.dt.uint32
+U16 = mybir.dt.uint16
+U8 = mybir.dt.uint8
+FP8X4 = mybir.dt.float8_e4m3fn_x4
+FP4X4 = mybir.dt.float4_e2m1fn_x4
+COPY = mybir.ActivationFunctionType.Copy
+ADD = mybir.AluOpType.add
+MULT = mybir.AluOpType.mult
+
+P = 128
+PACK = 4
+BANK = 512
+HALF = I // 2
+LIST_COLS = I // 16
+
+
+def load_scale_rows(queues, plane, scales):
+    for r in range(4):
+        queues[r].dma_start(out=plane[r:P:32, :].bitcast(I32), in_=scales[0][r:16:4, :].bitcast(I32))
+
+
+def tile_attend_pagesintonotes_kernel(tc, pages_words, pages_scales, wa_words, wa_scales, notes_words, notes_scales,
+                                       wb_words, wb_scales, kf, wo_words, wo_scales, offs, offs2, offs3, out):
+    nc = tc.nc
+    with ExitStack() as ctx:
+        keep = ctx.enter_context(tc.tile_pool(name="keep", bufs=1))
+        reuse = ctx.enter_context(tc.tile_pool(name="reuse", bufs=1))
+        psum = ctx.enter_context(tc.psum_pool(name="psum", bufs=8))
+
+        list_pages = keep.tile([P, LIST_COLS], U16, name="list_pages")
+        list_put = keep.tile([P, LIST_COLS], U16, name="list_put")
+        list_get = keep.tile([P, LIST_COLS], U16, name="list_get")
+        pool_words = keep.tile([P, T], U32, name="pool_words", align_bytes=64)
+        pool_scales = keep.tile([P, T], U8, name="pool_scales", align_bytes=64)
+        page_words = keep.tile([P, I], U32, name="page_words", align_bytes=64)
+        page_scales = keep.tile([P, I], U8, name="page_scales", align_bytes=64)
+        stage = keep.tile([P, 4096], U8, name="stage", align_bytes=64)
+        wa_raw = stage[:, 1536:2560]
+        wb_raw = stage[:, 0:2048]
+        notes = stage[:, 2048:4096]
+        wo = stage[:, 0:512]
+        wa_plane_raw = reuse.tile([P, K], U8, name="wa_plane_raw", offset=4 * U - K // 2)
+        planes = keep.tile([P, K + U + E], U8, name="planes", align_bytes=64)
+        wb_plane_raw = planes[:, 0:K]
+        notes_plane = planes[:, K:K + U]
+        wo_plane = planes[:, K + U:K + U + E]
+        wa = keep.tile([P, 2 * K], U8, name="wa", align_bytes=64)
+        wa_plane = keep.tile([P, K], U8, name="wa_plane", align_bytes=64)
+        wb = keep.tile([P, K], U32, name="wb", align_bytes=64)
+        wb_plane = keep.tile([P, K], U8, name="wb_plane", align_bytes=64)
+        factor = keep.tile([P, PACK], F32, name="factor")
+        z = [keep.tile([P, I], F32, name=f"z{j}") for j in range(PACK)]
+        f1 = [keep.tile([P, U], F32, name=f"f1_{j}") for j in (0, 1)]
+        f1 = f1 + [reuse.tile([P, U], F32, name=f"f1_{j}", offset=4 * U * (j - 2)) for j in (2, 3)]
+        factor4 = keep.tile([P, PACK, 4], F32, name="factor4")
+        c1 = [keep.tile([P, U], F32, name=f"c1_{j}") for j in range(PACK)]
+        picked = [keep.tile([P, PACK, HALF], F32, name=f"picked{h}") for h in range(2)]
+        w = [keep.tile([P, HALF, PACK], BF16, name=f"w{h}", align_bytes=64) for h in range(2)]
+        w_words = [keep.tile([P, HALF], U32, name=f"w_words{h}", align_bytes=64) for h in range(2)]
+        w_plane = [keep.tile([P, HALF], U8, name=f"w_plane{h}", align_bytes=64) for h in range(2)]
+        result = [[keep.tile([P, HALF], F32, name=f"result{h}{t}") for t in range(2)] for h in range(2)]
+
+        nc.vector.memset(pool_scales[:].bitcast(I32), 0)
+        nc.vector.memset(wa_plane_raw[:].bitcast(I32), 0)
+
+        nc.sync.dma_start(list_pages[:], offs)
+        nc.sync.dma_start(list_put[:], offs2)
+        nc.sync.dma_start(list_get[:], offs3)
+        nc.sync.dma_start(out=pool_words[:].bitcast(I32), in_=pages_words[0].rearrange("p n t -> p (n t)").bitcast(I32))
+        load_scale_rows([nc.scalar] * 4, pool_scales, pages_scales)
+        nc.gpsimd.dma_start(out=factor[:], in_=kf.rearrange("(p j) o -> p (j o)", j=PACK))
+        nc.gpsimd.dma_start(out=wa_raw.bitcast(I32), in_=wa_words[0].bitcast(I32))
+        load_scale_rows([nc.scalar, nc.scalar, nc.scalar, nc.gpsimd], wa_plane_raw, wa_scales)
+        nc.scalar.activation(factor4[:], factor[:].rearrange("p (j i) -> p j i", i=1).to_broadcast([P, PACK, 4]), COPY)
+
+        nc.vector.tensor_copy(page_scales[:], pool_scales[:].indirect(list_pages[:]))
+        nc.scalar.copy(out=wa[:].bitcast(U16).rearrange("p (j m) -> p j m", j=PACK),
+                       in_=wa_raw.bitcast(U16).rearrange("p (m j) -> p j m", j=PACK))
+        nc.vector.tensor_copy(out=wa_plane[:].rearrange("p (j m) -> p j m", j=PACK),
+                              in_=wa_plane_raw[:].rearrange("p (m j) -> p j m", j=PACK))
+        for h in range(2):
+            nc.vector.tensor_copy(page_words[:, HALF * h:HALF * (h + 1)], pool_words[:].indirect(list_pages[:, 16 * h:16 * (h + 1)]))
+
+        for j in (0, 1):
+            nc.vector.memset(f1[j][:], 0.0)
+        for j in (2, 3):
+            nc.gpsimd.memset(f1[j][:], 0.0)
+        nc.vector.memset(planes[:].bitcast(I32), 0)
+
+        nc.sync.dma_start(out=wb_raw.bitcast(I32), in_=wb_words[0].rearrange("p n t -> p (n t)").bitcast(I32))
+        load_scale_rows([nc.sync] * 4, wb_plane_raw, wb_scales)
+        nc.sync.dma_start(out=notes.bitcast(I32), in_=notes_words[0].bitcast(I32))
+        load_scale_rows([nc.sync] * 4, notes_plane, notes_scales)
+
+        def z_pass(j, lo, hi):
+            bank = psum.tile([P, BANK], F32, name=f"z_bank{j}_{lo}", tag="bank")
+            nc.tensor.matmul_mx(out=bank[:, 0:hi - lo], lhsT=wa[:, 2 * P * j:2 * P * (j + 1)].bitcast(FP4X4),
+                                lhsT_scale=wa_plane[:, P * j:P * (j + 1)],
+                                rhs=page_words[:, lo:hi].bitcast(FP8X4), rhs_scale=page_scales[:, lo:hi], start=True, stop=True)
+            return bank[:, 0:hi - lo]
+
+        def put_scalar(j, h):
+            nc.scalar.activation(f1[j][:].indirect(list_put[:, 16 * h:16 * (h + 1)]), z[j][:, HALF * h:HALF * (h + 1)], COPY)
+
+        for h in range(2):
+            cols = slice(HALF * h, HALF * (h + 1))
+            nc.scalar.copy(out=z[1][:, cols], in_=z_pass(1, cols.start, cols.stop))
+            nc.vector.tensor_copy(out=z[0][:, cols], in_=z_pass(0, cols.start, cols.stop))
+            if h == 0:
+                put_scalar(1, 0)
+            nc.vector.tensor_copy(f1[0][:].indirect(list_put[:, 16 * h:16 * (h + 1)]), z[0][:, cols])
+        nc.scalar.copy(out=z[2][:], in_=z_pass(2, 0, I))
+        put_scalar(1, 1)
+        nc.vector.tensor_copy(f1[2][:].indirect(list_put[:]), z[2][:])
+        nc.scalar.copy(out=z[3][:], in_=z_pass(3, 0, I))
+        put_scalar(3, 0)
+        put_scalar(3, 1)
+
+        nc.gpsimd.tensor_copy(out=wb[:].bitcast(I32).rearrange("p (j m) -> p j m", j=PACK),
+                              in_=wb_raw.bitcast(I32).rearrange("p (m j) -> p j m", j=PACK))
+        nc.gpsimd.tensor_copy(out=wb_plane[:].rearrange("p (j m) -> p j m", j=PACK),
+                              in_=wb_plane_raw.rearrange("p (m j) -> p j m", j=PACK))
+        nc.sync.dma_start(out=wo.bitcast(I32), in_=wo_words[0].bitcast(I32))
+        load_scale_rows([nc.sync] * 4, wo_plane, wo_scales)
+
+        for j in (0, 2, 1, 3):
+            for u in range(U // BANK):
+                bank = psum.tile([P, BANK], F32, name=f"h_bank{j}{u}", tag="bank")
+                nc.tensor.matmul_mx(out=bank[:], lhsT=wb[:, P * j:P * (j + 1)].bitcast(FP8X4),
+                                    lhsT_scale=wb_plane[:, P * j:P * (j + 1)],
+                                    rhs=notes[:, 2 * BANK * u:2 * BANK * (u + 1)].bitcast(FP4X4),
+                                    rhs_scale=notes_plane[:, BANK * u:BANK * (u + 1)], start=True, stop=True)
+                nc.vector.tensor_tensor(out=c1[j][:, BANK * u:BANK * (u + 1)], in0=bank[:],
+                                        in1=f1[j][:, BANK * u:BANK * (u + 1)], op=ADD)
+
+        for h in range(2):
+            for j in (0, 2, 1, 3):
+                window = c1[j][:].indirect(list_get[:, 16 * h:16 * (h + 1)])
+                if (h, j) == (0, 3):
+                    nc.vector.tensor_copy(picked[h][:, j, :], window)
+                else:
+                    nc.scalar.activation(picked[h][:, j, :], window, COPY)
+
+        spread = factor4[:].rearrange("p (c j) i -> p c j i", c=1).to_broadcast([P, HALF // 4, PACK, 4])
+        for h in range(2):
+            nc.vector.tensor_tensor(out=w[h][:].rearrange("p (c i) j -> p c j i", i=4),
+                                    in0=picked[h][:].rearrange("p j (c i) -> p c j i", i=4), in1=spread, op=MULT)
+            nc.vector.quantize_mx(out=w_words[h][:].bitcast(FP8X4), scales=w_plane[h][:],
+                                  in_=w[h][:].rearrange("p i j -> p (i j)"))
+            for t in range(E // P):
+                bank = psum.tile([P, BANK], F32, name=f"y_bank{h}{t}", tag="bank")
+                nc.tensor.matmul_mx(out=bank[:, 0:HALF], lhsT=wo[:, 2 * P * t:2 * P * (t + 1)].bitcast(FP4X4),
+                                    lhsT_scale=wo_plane[:, P * t:P * (t + 1)],
+                                    rhs=w_words[h][:].bitcast(FP8X4), rhs_scale=w_plane[h][:], start=True, stop=True)
+                if (h, t) == (1, 1):
+                    nc.vector.tensor_copy(out=result[h][t][:], in_=bank[:, 0:HALF])
+                else:
+                    nc.scalar.copy(out=result[h][t][:], in_=bank[:, 0:HALF])
+                nc.sync.dma_start(out=out[P * t:P * (t + 1), HALF * h:HALF * (h + 1)], in_=result[h][t][:])

@@ -24,9 +24,9 @@ HALF = I // 2
 LIST_COLS = I // 16
 
 
-def load_scale_rows(queues, plane, scales):
+def load_scale_rows(nc, plane, scales):
     for r in range(4):
-        queues[r].dma_start(out=plane[r:P:32, :].bitcast(I32), in_=scales[0][r:16:4, :].bitcast(I32))
+        nc.sync.dma_start(out=plane[r:P:32, :].bitcast(I32), in_=scales[0][r:16:4, :].bitcast(I32))
 
 
 def tile_attend_pagesintonotes_kernel(tc, pages_words, pages_scales, wa_words, wa_scales, notes_words, notes_scales,
@@ -35,7 +35,7 @@ def tile_attend_pagesintonotes_kernel(tc, pages_words, pages_scales, wa_words, w
     with ExitStack() as ctx:
         keep = ctx.enter_context(tc.tile_pool(name="keep", bufs=1))
         reuse = ctx.enter_context(tc.tile_pool(name="reuse", bufs=1))
-        psum = ctx.enter_context(tc.psum_pool(name="psum", bufs=8))
+        psum = ctx.enter_context(tc.psum_pool(name="psum", bufs=1))
 
         list_pages = keep.tile([P, LIST_COLS], U16, name="list_pages")
         list_put = keep.tile([P, LIST_COLS], U16, name="list_put")
@@ -44,25 +44,30 @@ def tile_attend_pagesintonotes_kernel(tc, pages_words, pages_scales, wa_words, w
         pool_scales = keep.tile([P, T], U8, name="pool_scales", align_bytes=64)
         page_words = keep.tile([P, I], U32, name="page_words", align_bytes=64)
         page_scales = keep.tile([P, I], U8, name="page_scales", align_bytes=64)
-        stage = keep.tile([P, 4096], U8, name="stage", align_bytes=64)
-        wa_raw = stage[:, 1536:2560]
-        wb_raw = stage[:, 0:2048]
-        notes = stage[:, 2048:4096]
-        wo = stage[:, 0:512]
-        wa_plane_raw = reuse.tile([P, K], U8, name="wa_plane_raw", offset=4 * U - K // 2)
-        planes = keep.tile([P, K + U + E], U8, name="planes", align_bytes=64)
-        wb_plane_raw = planes[:, 0:K]
-        notes_plane = planes[:, K:K + U]
-        wo_plane = planes[:, K + U:K + U + E]
+        wa_raw = keep.tile([P, 2 * K], U8, name="wa_raw")
+        notes = keep.tile([P, 2 * U], U8, name="notes", align_bytes=64)
+        wo = keep.tile([P, 2 * E], U8, name="wo", align_bytes=64)
+        planes = keep.tile([P, U + E], U8, name="planes", align_bytes=64)
+        notes_plane = planes[:, 0:U]
+        wo_plane = planes[:, U:U + E]
         wa = keep.tile([P, 2 * K], U8, name="wa", align_bytes=64)
         wa_plane = keep.tile([P, K], U8, name="wa_plane", align_bytes=64)
         wb = keep.tile([P, K], U32, name="wb", align_bytes=64)
         wb_plane = keep.tile([P, K], U8, name="wb_plane", align_bytes=64)
         factor = keep.tile([P, PACK], F32, name="factor")
-        z = [keep.tile([P, I], F32, name=f"z{j}") for j in range(PACK)]
+        factor4 = keep.tile([P, PACK, 4], F32, name="factor4")
+        wa_plane_raw = reuse.tile([P, K], U8, name="wa_plane_raw", offset=4 * U - K // 2)
+        wb_plane_raw = reuse.tile([P, K], U8, name="wb_plane_raw", offset=8 * U)
+        wb_raw = reuse.tile([P, K], I32, name="wb_raw", offset=9 * U)
         f1 = [keep.tile([P, U], F32, name=f"f1_{j}") for j in (0, 1)]
         f1 = f1 + [reuse.tile([P, U], F32, name=f"f1_{j}", offset=4 * U * (j - 2)) for j in (2, 3)]
-        factor4 = keep.tile([P, PACK, 4], F32, name="factor4")
+        z = {(j, 0): keep.tile([P, HALF], F32, name=f"z{j}a") for j in (0, 1)}
+        z[0, 1] = reuse.tile([P, HALF], F32, name="z0b", offset=8 * U)
+        z12 = reuse.tile([P, I], F32, name="z12", offset=9 * U)
+        z23 = keep.tile([P, I], F32, name="z23")
+        z[1, 1], z[2, 0] = z12[:, 0:HALF], z12[:, HALF:I]
+        z[2, 1], z[3, 0] = z23[:, 0:HALF], z23[:, HALF:I]
+        z[3, 1] = keep.tile([P, HALF], F32, name="z3b")
         c1 = [keep.tile([P, U], F32, name=f"c1_{j}") for j in range(PACK)]
         picked = [keep.tile([P, PACK, HALF], F32, name=f"picked{h}") for h in range(2)]
         w = [keep.tile([P, HALF, PACK], BF16, name=f"w{h}", align_bytes=64) for h in range(2)]
@@ -70,86 +75,99 @@ def tile_attend_pagesintonotes_kernel(tc, pages_words, pages_scales, wa_words, w
         w_plane = [keep.tile([P, HALF], U8, name=f"w_plane{h}", align_bytes=64) for h in range(2)]
         result = [[keep.tile([P, HALF], F32, name=f"result{h}{t}") for t in range(2)] for h in range(2)]
 
+        def half(h):
+            return slice(HALF * h, HALF * (h + 1))
+
+        def list_half(listed, h):
+            return listed[:, LIST_COLS // 2 * h:LIST_COLS // 2 * (h + 1)]
+
         nc.vector.memset(pool_scales[:].bitcast(I32), 0)
         nc.vector.memset(wa_plane_raw[:].bitcast(I32), 0)
+        nc.vector.memset(wb_plane_raw[:].bitcast(I32), 0)
+        nc.vector.memset(planes[:].bitcast(I32), 0)
 
-        nc.sync.dma_start(list_pages[:], offs)
-        nc.sync.dma_start(list_put[:], offs2)
-        nc.sync.dma_start(list_get[:], offs3)
-        nc.sync.dma_start(out=pool_words[:].bitcast(I32), in_=pages_words[0].rearrange("p n t -> p (n t)").bitcast(I32))
-        load_scale_rows([nc.scalar] * 4, pool_scales, pages_scales)
+        pages_rows = pages_words[0].rearrange("p n t -> p (n t)").bitcast(I32)
         nc.gpsimd.dma_start(out=factor[:], in_=kf.rearrange("(p j) o -> p (j o)", j=PACK))
-        nc.gpsimd.dma_start(out=wa_raw.bitcast(I32), in_=wa_words[0].bitcast(I32))
-        load_scale_rows([nc.scalar, nc.scalar, nc.scalar, nc.gpsimd], wa_plane_raw, wa_scales)
-        nc.scalar.activation(factor4[:], factor[:].rearrange("p (j i) -> p j i", i=1).to_broadcast([P, PACK, 4]), COPY)
+        nc.sync.dma_start(list_pages[:], offs)
+        nc.sync.dma_start(out=wa_raw[:].bitcast(I32), in_=wa_words[0].bitcast(I32))
+        nc.sync.dma_start(out=pool_words[:, 0:T // 2].bitcast(I32), in_=pages_rows[:, 0:T // 2])
+        load_scale_rows(nc, pool_scales, pages_scales)
+        nc.sync.dma_start(out=pool_words[:, T // 2:T].bitcast(I32), in_=pages_rows[:, T // 2:T])
+        load_scale_rows(nc, wa_plane_raw, wa_scales)
+        nc.sync.dma_start(out=wb_raw[:], in_=wb_words[0].rearrange("p n t -> p (n t)").bitcast(I32))
+        nc.sync.dma_start(list_put[:], offs2)
+        load_scale_rows(nc, wb_plane_raw, wb_scales)
+        nc.sync.dma_start(out=notes[:].bitcast(I32), in_=notes_words[0].bitcast(I32))
+        load_scale_rows(nc, notes_plane, notes_scales)
+        nc.sync.dma_start(list_get[:], offs3)
+        nc.sync.dma_start(out=wo[:].bitcast(I32), in_=wo_words[0].bitcast(I32))
+        load_scale_rows(nc, wo_plane, wo_scales)
 
+        nc.scalar.activation(factor4[:], factor[:].rearrange("p (j i) -> p j i", i=1).to_broadcast([P, PACK, 4]), COPY)
         nc.vector.tensor_copy(page_scales[:], pool_scales[:].indirect(list_pages[:]))
         nc.scalar.copy(out=wa[:].bitcast(U16).rearrange("p (j m) -> p j m", j=PACK),
-                       in_=wa_raw.bitcast(U16).rearrange("p (m j) -> p j m", j=PACK))
+                       in_=wa_raw[:].bitcast(U16).rearrange("p (m j) -> p j m", j=PACK))
         nc.vector.tensor_copy(out=wa_plane[:].rearrange("p (j m) -> p j m", j=PACK),
                               in_=wa_plane_raw[:].rearrange("p (m j) -> p j m", j=PACK))
         for h in range(2):
-            nc.vector.tensor_copy(page_words[:, HALF * h:HALF * (h + 1)], pool_words[:].indirect(list_pages[:, 16 * h:16 * (h + 1)]))
+            nc.vector.tensor_copy(page_words[:, half(h)], pool_words[:].indirect(list_half(list_pages, h)))
 
-        for j in (0, 1):
-            nc.vector.memset(f1[j][:], 0.0)
-        for j in (2, 3):
+        for j in (1, 0, 2, 3):
             nc.gpsimd.memset(f1[j][:], 0.0)
-        nc.vector.memset(planes[:].bitcast(I32), 0)
 
-        nc.sync.dma_start(out=wb_raw.bitcast(I32), in_=wb_words[0].rearrange("p n t -> p (n t)").bitcast(I32))
-        load_scale_rows([nc.sync] * 4, wb_plane_raw, wb_scales)
-        nc.sync.dma_start(out=notes.bitcast(I32), in_=notes_words[0].bitcast(I32))
-        load_scale_rows([nc.sync] * 4, notes_plane, notes_scales)
+        def z_bank(number, parts):
+            bank = psum.tile([P, BANK], F32, name=f"z_bank{number}", tag=f"bank{number}")
+            for place, (j, h) in enumerate(parts):
+                nc.tensor.matmul_mx(out=bank[:, half(place)], lhsT=wa[:, 2 * P * j:2 * P * (j + 1)].bitcast(FP4X4),
+                                    lhsT_scale=wa_plane[:, P * j:P * (j + 1)],
+                                    rhs=page_words[:, half(h)].bitcast(FP8X4), rhs_scale=page_scales[:, half(h)],
+                                    start=True, stop=True)
+            return bank[:, 0:HALF * len(parts)]
 
-        def z_pass(j, lo, hi):
-            bank = psum.tile([P, BANK], F32, name=f"z_bank{j}_{lo}", tag="bank")
-            nc.tensor.matmul_mx(out=bank[:, 0:hi - lo], lhsT=wa[:, 2 * P * j:2 * P * (j + 1)].bitcast(FP4X4),
-                                lhsT_scale=wa_plane[:, P * j:P * (j + 1)],
-                                rhs=page_words[:, lo:hi].bitcast(FP8X4), rhs_scale=page_scales[:, lo:hi], start=True, stop=True)
-            return bank[:, 0:hi - lo]
+        def put_vector(j, h):
+            nc.vector.tensor_copy(f1[j][:].indirect(list_half(list_put, h)), z[j, h][:])
 
         def put_scalar(j, h):
-            nc.scalar.activation(f1[j][:].indirect(list_put[:, 16 * h:16 * (h + 1)]), z[j][:, HALF * h:HALF * (h + 1)], COPY)
+            nc.scalar.activation(f1[j][:].indirect(list_half(list_put, h)), z[j, h][:], COPY)
 
-        for h in range(2):
-            cols = slice(HALF * h, HALF * (h + 1))
-            nc.scalar.copy(out=z[1][:, cols], in_=z_pass(1, cols.start, cols.stop))
-            nc.vector.tensor_copy(out=z[0][:, cols], in_=z_pass(0, cols.start, cols.stop))
-            if h == 0:
-                put_scalar(1, 0)
-            nc.vector.tensor_copy(f1[0][:].indirect(list_put[:, 16 * h:16 * (h + 1)]), z[0][:, cols])
-        nc.scalar.copy(out=z[2][:], in_=z_pass(2, 0, I))
+        nc.scalar.copy(out=z[1, 0][:], in_=z_bank(0, [(1, 0)]))
+        nc.vector.tensor_copy(out=z[0, 0][:], in_=z_bank(1, [(0, 0)]))
+        put_scalar(1, 0)
+        put_vector(0, 0)
+
+        nc.scalar.copy(out=wb[:].rearrange("p (j m) -> p m j", j=PACK),
+                       in_=wb_raw[:].bitcast(U32).rearrange("p (m j) -> p m j", j=PACK))
+        nc.vector.tensor_copy(out=wb_plane[:].rearrange("p (j m) -> p j m", j=PACK),
+                              in_=wb_plane_raw[:].rearrange("p (m j) -> p j m", j=PACK))
+
+        nc.vector.tensor_copy(out=z[0, 1][:], in_=z_bank(2, [(0, 1)]))
+        nc.scalar.copy(out=z12[:], in_=z_bank(3, [(1, 1), (2, 0)]))
+        put_vector(0, 1)
         put_scalar(1, 1)
-        nc.vector.tensor_copy(f1[2][:].indirect(list_put[:]), z[2][:])
-        nc.scalar.copy(out=z[3][:], in_=z_pass(3, 0, I))
+        nc.scalar.copy(out=z23[:], in_=z_bank(4, [(2, 1), (3, 0)]))
+        put_vector(2, 0)
+        put_scalar(2, 1)
         put_scalar(3, 0)
+        nc.scalar.copy(out=z[3, 1][:], in_=z_bank(5, [(3, 1)]))
         put_scalar(3, 1)
 
-        nc.gpsimd.tensor_copy(out=wb[:].bitcast(I32).rearrange("p (j m) -> p j m", j=PACK),
-                              in_=wb_raw.bitcast(I32).rearrange("p (m j) -> p j m", j=PACK))
-        nc.gpsimd.tensor_copy(out=wb_plane[:].rearrange("p (j m) -> p j m", j=PACK),
-                              in_=wb_plane_raw.rearrange("p (m j) -> p j m", j=PACK))
-        nc.sync.dma_start(out=wo.bitcast(I32), in_=wo_words[0].bitcast(I32))
-        load_scale_rows([nc.sync] * 4, wo_plane, wo_scales)
+        def look_up(j, h):
+            return c1[j][:].indirect(list_half(list_get, h))
 
-        for j in (0, 2, 1, 3):
+        for j in range(PACK):
+            if j == PACK - 1:
+                nc.vector.tensor_copy(picked[0][:, 0, :], look_up(0, 0))
             for u in range(U // BANK):
-                bank = psum.tile([P, BANK], F32, name=f"h_bank{j}{u}", tag="bank")
+                bank = psum.tile([P, BANK], F32, name=f"h_bank{j}{u}", tag=f"bank{(6 + 2 * j + u) % 8}")
                 nc.tensor.matmul_mx(out=bank[:], lhsT=wb[:, P * j:P * (j + 1)].bitcast(FP8X4),
                                     lhsT_scale=wb_plane[:, P * j:P * (j + 1)],
                                     rhs=notes[:, 2 * BANK * u:2 * BANK * (u + 1)].bitcast(FP4X4),
                                     rhs_scale=notes_plane[:, BANK * u:BANK * (u + 1)], start=True, stop=True)
                 nc.vector.tensor_tensor(out=c1[j][:, BANK * u:BANK * (u + 1)], in0=bank[:],
                                         in1=f1[j][:, BANK * u:BANK * (u + 1)], op=ADD)
-
-        for h in range(2):
-            for j in (0, 2, 1, 3):
-                window = c1[j][:].indirect(list_get[:, 16 * h:16 * (h + 1)])
-                if (h, j) == (0, 3):
-                    nc.vector.tensor_copy(picked[h][:, j, :], window)
-                else:
-                    nc.scalar.activation(picked[h][:, j, :], window, COPY)
+        nc.vector.tensor_copy(picked[0][:, 3, :], look_up(3, 0))
+        for j, h in ((1, 0), (2, 0), (0, 1), (1, 1), (2, 1), (3, 1)):
+            nc.scalar.activation(picked[h][:, j, :], look_up(j, h), COPY)
 
         spread = factor4[:].rearrange("p (c j) i -> p c j i", c=1).to_broadcast([P, HALF // 4, PACK, 4])
         for h in range(2):
@@ -158,7 +176,7 @@ def tile_attend_pagesintonotes_kernel(tc, pages_words, pages_scales, wa_words, w
             nc.vector.quantize_mx(out=w_words[h][:].bitcast(FP8X4), scales=w_plane[h][:],
                                   in_=w[h][:].rearrange("p i j -> p (i j)"))
             for t in range(E // P):
-                bank = psum.tile([P, BANK], F32, name=f"y_bank{h}{t}", tag="bank")
+                bank = psum.tile([P, BANK], F32, name=f"y_bank{h}{t}", tag=f"bank{(6 + 2 * h + t) % 8}")
                 nc.tensor.matmul_mx(out=bank[:, 0:HALF], lhsT=wo[:, 2 * P * t:2 * P * (t + 1)].bitcast(FP4X4),
                                     lhsT_scale=wo_plane[:, P * t:P * (t + 1)],
                                     rhs=w_words[h][:].bitcast(FP8X4), rhs_scale=w_plane[h][:], start=True, stop=True)
@@ -166,4 +184,4 @@ def tile_attend_pagesintonotes_kernel(tc, pages_words, pages_scales, wa_words, w
                     nc.vector.tensor_copy(out=result[h][t][:], in_=bank[:, 0:HALF])
                 else:
                     nc.scalar.copy(out=result[h][t][:], in_=bank[:, 0:HALF])
-                nc.sync.dma_start(out=out[P * t:P * (t + 1), HALF * h:HALF * (h + 1)], in_=result[h][t][:])
+                nc.sync.dma_start(out=out[P * t:P * (t + 1), half(h)], in_=result[h][t][:])

@@ -24,9 +24,9 @@ HALF = I // 2
 LIST_COLS = I // 16
 
 
-def load_scale_rows(nc, plane, scales):
-    for r in range(4):
-        nc.sync.dma_start(out=plane[r:P:32, :].bitcast(I32), in_=scales[0][r:16:4, :].bitcast(I32))
+def load_scale_rows(queues, plane, scales):
+    for r, queue in enumerate(queues):
+        queue.dma_start(out=plane[r:P:32, :].bitcast(I32), in_=scales[0][r:16:4, :].bitcast(I32))
 
 
 def tile_attend_pagesintonotes_kernel(tc, pages_words, pages_scales, wa_words, wa_scales, notes_words, notes_scales,
@@ -42,7 +42,6 @@ def tile_attend_pagesintonotes_kernel(tc, pages_words, pages_scales, wa_words, w
         list_get = keep.tile([P, LIST_COLS], U16, name="list_get")
         pool_words = keep.tile([P, T], U32, name="pool_words", align_bytes=64)
         pool_scales = keep.tile([P, T], U8, name="pool_scales", align_bytes=64)
-        page_words = keep.tile([P, I], U32, name="page_words", align_bytes=64)
         page_scales = keep.tile([P, I], U8, name="page_scales", align_bytes=64)
         wa_raw = keep.tile([P, 2 * K], U8, name="wa_raw")
         notes = keep.tile([P, 2 * U], U8, name="notes", align_bytes=64)
@@ -55,19 +54,19 @@ def tile_attend_pagesintonotes_kernel(tc, pages_words, pages_scales, wa_words, w
         wb = keep.tile([P, K], U32, name="wb", align_bytes=64)
         wb_plane = keep.tile([P, K], U8, name="wb_plane", align_bytes=64)
         factor = keep.tile([P, PACK], F32, name="factor")
-        factor4 = keep.tile([P, PACK, 4], F32, name="factor4")
-        wa_plane_raw = reuse.tile([P, K], U8, name="wa_plane_raw", offset=4 * U - K // 2)
-        wb_plane_raw = reuse.tile([P, K], U8, name="wb_plane_raw", offset=8 * U)
-        wb_raw = reuse.tile([P, K], I32, name="wb_raw", offset=9 * U)
+        page_words = [reuse.tile([P, HALF], U32, name="page_words0", align_bytes=64, offset=0),
+                      reuse.tile([P, HALF], U32, name="page_words1", align_bytes=64, offset=4 * U)]
+        wa_plane_raw = reuse.tile([P, K], U8, name="wa_plane_raw", offset=4 * U + 4 * HALF - K // 2)
         f1 = [keep.tile([P, U], F32, name=f"f1_{j}") for j in (0, 1)]
-        f1 = f1 + [reuse.tile([P, U], F32, name=f"f1_{j}", offset=4 * U * (j - 2)) for j in (2, 3)]
-        z = {(j, 0): keep.tile([P, HALF], F32, name=f"z{j}a") for j in (0, 1)}
-        z[0, 1] = reuse.tile([P, HALF], F32, name="z0b", offset=8 * U)
-        z12 = reuse.tile([P, I], F32, name="z12", offset=9 * U)
-        z23 = keep.tile([P, I], F32, name="z23")
-        z[1, 1], z[2, 0] = z12[:, 0:HALF], z12[:, HALF:I]
-        z[2, 1], z[3, 0] = z23[:, 0:HALF], z23[:, HALF:I]
-        z[3, 1] = keep.tile([P, HALF], F32, name="z3b")
+        f1.append(reuse.tile([P, U], F32, name="f1_2", offset=4 * U + 4 * HALF))
+        f1.append(reuse.tile([P, U], F32, name="f1_3", offset=0))
+        wb_plane_raw = keep.tile([P, K], U8, name="wb_plane_raw")
+        wb_raw = keep.tile([P, K], I32, name="wb_raw")
+        z0a = keep.tile([P, HALF], F32, name="z0a")
+        z1a = keep.tile([P, HALF], F32, name="z1a")
+        z10b = keep.tile([P, I], F32, name="z10b")
+        z2 = keep.tile([P, I], F32, name="z2")
+        z3 = keep.tile([P, I], F32, name="z3")
         c1 = [keep.tile([P, U], F32, name=f"c1_{j}") for j in range(PACK)]
         picked = [keep.tile([P, PACK, HALF], F32, name=f"picked{h}") for h in range(2)]
         w = [keep.tile([P, HALF, PACK], BF16, name=f"w{h}", align_bytes=64) for h in range(2)]
@@ -82,83 +81,77 @@ def tile_attend_pagesintonotes_kernel(tc, pages_words, pages_scales, wa_words, w
             return listed[:, LIST_COLS // 2 * h:LIST_COLS // 2 * (h + 1)]
 
         nc.vector.memset(pool_scales[:].bitcast(I32), 0)
-        nc.vector.memset(wa_plane_raw[:].bitcast(I32), 0)
+        nc.gpsimd.memset(wa_plane_raw[:].bitcast(I32), 0)
         nc.vector.memset(wb_plane_raw[:].bitcast(I32), 0)
         nc.vector.memset(planes[:].bitcast(I32), 0)
 
         pages_rows = pages_words[0].rearrange("p n t -> p (n t)").bitcast(I32)
-        nc.gpsimd.dma_start(out=factor[:], in_=kf.rearrange("(p j) o -> p (j o)", j=PACK))
         nc.sync.dma_start(list_pages[:], offs)
         nc.sync.dma_start(out=wa_raw[:].bitcast(I32), in_=wa_words[0].bitcast(I32))
-        nc.sync.dma_start(out=pool_words[:, 0:T // 2].bitcast(I32), in_=pages_rows[:, 0:T // 2])
-        load_scale_rows(nc, pool_scales, pages_scales)
-        nc.sync.dma_start(out=pool_words[:, T // 2:T].bitcast(I32), in_=pages_rows[:, T // 2:T])
-        load_scale_rows(nc, wa_plane_raw, wa_scales)
+        nc.sync.dma_start(out=pool_words[:, 0:T // 4].bitcast(I32), in_=pages_rows[:, 0:T // 4])
+        load_scale_rows([nc.sync] * 4, pool_scales, pages_scales)
+        nc.sync.dma_start(out=pool_words[:, T // 4:T].bitcast(I32), in_=pages_rows[:, T // 4:T])
+        load_scale_rows([nc.sync, nc.sync, nc.sync, nc.gpsimd], wa_plane_raw, wa_scales)
         nc.sync.dma_start(out=wb_raw[:], in_=wb_words[0].rearrange("p n t -> p (n t)").bitcast(I32))
         nc.sync.dma_start(list_put[:], offs2)
-        load_scale_rows(nc, wb_plane_raw, wb_scales)
+        load_scale_rows([nc.sync] * 4, wb_plane_raw, wb_scales)
         nc.sync.dma_start(out=notes[:].bitcast(I32), in_=notes_words[0].bitcast(I32))
-        load_scale_rows(nc, notes_plane, notes_scales)
+        load_scale_rows([nc.sync] * 4, notes_plane, notes_scales)
         nc.sync.dma_start(list_get[:], offs3)
+        nc.sync.dma_start(out=factor[:], in_=kf.rearrange("(p j) o -> p (j o)", j=PACK))
         nc.sync.dma_start(out=wo[:].bitcast(I32), in_=wo_words[0].bitcast(I32))
-        load_scale_rows(nc, wo_plane, wo_scales)
+        load_scale_rows([nc.sync] * 4, wo_plane, wo_scales)
 
-        nc.scalar.activation(factor4[:], factor[:].rearrange("p (j i) -> p j i", i=1).to_broadcast([P, PACK, 4]), COPY)
         nc.vector.tensor_copy(page_scales[:], pool_scales[:].indirect(list_pages[:]))
         nc.scalar.copy(out=wa[:].bitcast(U16).rearrange("p (j m) -> p j m", j=PACK),
                        in_=wa_raw[:].bitcast(U16).rearrange("p (m j) -> p j m", j=PACK))
+        nc.vector.tensor_copy(page_words[0][:], pool_words[:].indirect(list_half(list_pages, 0)))
         nc.vector.tensor_copy(out=wa_plane[:].rearrange("p (j m) -> p j m", j=PACK),
                               in_=wa_plane_raw[:].rearrange("p (m j) -> p j m", j=PACK))
-        for h in range(2):
-            nc.vector.tensor_copy(page_words[:, half(h)], pool_words[:].indirect(list_half(list_pages, h)))
+        nc.vector.tensor_copy(page_words[1][:], pool_words[:].indirect(list_half(list_pages, 1)))
 
-        for j in (1, 0, 2, 3):
+        for j in (1, 0, 2):
             nc.gpsimd.memset(f1[j][:], 0.0)
+        nc.gpsimd.tensor_copy(out=wb[:].bitcast(I32).rearrange("p (j m) -> p j m", j=PACK),
+                              in_=wb_raw[:].rearrange("p (m j) -> p j m", j=PACK))
+        nc.gpsimd.tensor_copy(out=wb_plane[:].rearrange("p (j m) -> p j m", j=PACK),
+                              in_=wb_plane_raw[:].rearrange("p (m j) -> p j m", j=PACK))
 
         def z_bank(number, parts):
             bank = psum.tile([P, BANK], F32, name=f"z_bank{number}", tag=f"bank{number}")
             for place, (j, h) in enumerate(parts):
                 nc.tensor.matmul_mx(out=bank[:, half(place)], lhsT=wa[:, 2 * P * j:2 * P * (j + 1)].bitcast(FP4X4),
                                     lhsT_scale=wa_plane[:, P * j:P * (j + 1)],
-                                    rhs=page_words[:, half(h)].bitcast(FP8X4), rhs_scale=page_scales[:, half(h)],
+                                    rhs=page_words[h][:].bitcast(FP8X4), rhs_scale=page_scales[:, half(h)],
                                     start=True, stop=True)
             return bank[:, 0:HALF * len(parts)]
 
-        def put_vector(j, h):
-            nc.vector.tensor_copy(f1[j][:].indirect(list_half(list_put, h)), z[j, h][:])
+        def places(j, h):
+            return f1[j][:].indirect(list_half(list_put, h))
 
-        def put_scalar(j, h):
-            nc.scalar.activation(f1[j][:].indirect(list_half(list_put, h)), z[j, h][:], COPY)
-
-        nc.scalar.copy(out=z[1, 0][:], in_=z_bank(0, [(1, 0)]))
-        nc.vector.tensor_copy(out=z[0, 0][:], in_=z_bank(1, [(0, 0)]))
-        put_scalar(1, 0)
-        put_vector(0, 0)
-
-        nc.scalar.copy(out=wb[:].rearrange("p (j m) -> p m j", j=PACK),
-                       in_=wb_raw[:].bitcast(U32).rearrange("p (m j) -> p m j", j=PACK))
-        nc.vector.tensor_copy(out=wb_plane[:].rearrange("p (j m) -> p j m", j=PACK),
-                              in_=wb_plane_raw[:].rearrange("p (m j) -> p j m", j=PACK))
-
-        nc.vector.tensor_copy(out=z[0, 1][:], in_=z_bank(2, [(0, 1)]))
-        nc.scalar.copy(out=z12[:], in_=z_bank(3, [(1, 1), (2, 0)]))
-        put_vector(0, 1)
-        put_scalar(1, 1)
-        nc.scalar.copy(out=z23[:], in_=z_bank(4, [(2, 1), (3, 0)]))
-        put_vector(2, 0)
-        put_scalar(2, 1)
-        put_scalar(3, 0)
-        nc.scalar.copy(out=z[3, 1][:], in_=z_bank(5, [(3, 1)]))
-        put_scalar(3, 1)
+        nc.scalar.activation(z1a[:], z_bank(0, [(1, 0)]), COPY)
+        nc.vector.tensor_copy(out=z0a[:], in_=z_bank(1, [(0, 0)]))
+        nc.scalar.activation(places(1, 0), z1a[:], COPY)
+        nc.vector.tensor_copy(places(0, 0), z0a[:])
+        nc.scalar.copy(out=z10b[:], in_=z_bank(2, [(1, 1), (0, 1)]))
+        nc.vector.tensor_copy(out=z2[:], in_=z_bank(3, [(2, 0), (2, 1)]))
+        nc.scalar.activation(places(1, 1), z10b[:, half(0)], COPY)
+        nc.vector.tensor_copy(f1[2][:].indirect(list_put[:]), z2[:])
+        nc.scalar.activation(places(0, 1), z10b[:, half(1)], COPY)
+        nc.scalar.copy(out=z3[:], in_=z_bank(4, [(3, 0), (3, 1)]))
+        nc.gpsimd.memset(f1[3][:], 0.0)
+        for h in range(2):
+            nc.scalar.activation(places(3, h), z3[:, half(h)], COPY)
 
         def look_up(j, h):
             return c1[j][:].indirect(list_half(list_get, h))
 
-        for j in range(PACK):
-            if j == PACK - 1:
+        for n, j in enumerate((1, 2, 0, 3)):
+            if j == 3:
+                nc.vector.tensor_copy(picked[0][:, 2, :], look_up(2, 0))
                 nc.vector.tensor_copy(picked[0][:, 0, :], look_up(0, 0))
             for u in range(U // BANK):
-                bank = psum.tile([P, BANK], F32, name=f"h_bank{j}{u}", tag=f"bank{(6 + 2 * j + u) % 8}")
+                bank = psum.tile([P, BANK], F32, name=f"h_bank{j}{u}", tag=f"bank{(5 + 2 * n + u) % 8}")
                 nc.tensor.matmul_mx(out=bank[:], lhsT=wb[:, P * j:P * (j + 1)].bitcast(FP8X4),
                                     lhsT_scale=wb_plane[:, P * j:P * (j + 1)],
                                     rhs=notes[:, 2 * BANK * u:2 * BANK * (u + 1)].bitcast(FP4X4),
@@ -166,17 +159,17 @@ def tile_attend_pagesintonotes_kernel(tc, pages_words, pages_scales, wa_words, w
                 nc.vector.tensor_tensor(out=c1[j][:, BANK * u:BANK * (u + 1)], in0=bank[:],
                                         in1=f1[j][:, BANK * u:BANK * (u + 1)], op=ADD)
         nc.vector.tensor_copy(picked[0][:, 3, :], look_up(3, 0))
-        for j, h in ((1, 0), (2, 0), (0, 1), (1, 1), (2, 1), (3, 1)):
+        for j, h in ((1, 0), (1, 1), (2, 1), (0, 1), (3, 1)):
             nc.scalar.activation(picked[h][:, j, :], look_up(j, h), COPY)
 
-        spread = factor4[:].rearrange("p (c j) i -> p c j i", c=1).to_broadcast([P, HALF // 4, PACK, 4])
+        spread = factor[:].rearrange("p (c j i) -> p c j i", c=1, i=1).to_broadcast([P, HALF // 2, PACK, 2])
         for h in range(2):
-            nc.vector.tensor_tensor(out=w[h][:].rearrange("p (c i) j -> p c j i", i=4),
-                                    in0=picked[h][:].rearrange("p j (c i) -> p c j i", i=4), in1=spread, op=MULT)
+            nc.vector.tensor_tensor(out=w[h][:].rearrange("p (c i) j -> p c j i", i=2),
+                                    in0=picked[h][:].rearrange("p j (c i) -> p c j i", i=2), in1=spread, op=MULT)
             nc.vector.quantize_mx(out=w_words[h][:].bitcast(FP8X4), scales=w_plane[h][:],
                                   in_=w[h][:].rearrange("p i j -> p (i j)"))
             for t in range(E // P):
-                bank = psum.tile([P, BANK], F32, name=f"y_bank{h}{t}", tag=f"bank{(6 + 2 * h + t) % 8}")
+                bank = psum.tile([P, BANK], F32, name=f"y_bank{h}{t}", tag=f"bank{(5 + 2 * h + t) % 8}")
                 nc.tensor.matmul_mx(out=bank[:, 0:HALF], lhsT=wo[:, 2 * P * t:2 * P * (t + 1)].bitcast(FP4X4),
                                     lhsT_scale=wo_plane[:, P * t:P * (t + 1)],
                                     rhs=w_words[h][:].bitcast(FP8X4), rhs_scale=w_plane[h][:], start=True, stop=True)

@@ -51,16 +51,14 @@ def tile_attend_pagesintonotes_kernel(tc, pages_words, pages_scales, wa_words, w
         wo_plane = planes[:, U:U + E]
         wa = keep.tile([P, 2 * K], U8, name="wa", align_bytes=64)
         wa_plane = keep.tile([P, K], U8, name="wa_plane", align_bytes=64)
-        wb = keep.tile([P, K], U32, name="wb", align_bytes=64)
         wb_plane = keep.tile([P, K], U8, name="wb_plane", align_bytes=64)
         factor = keep.tile([P, PACK], F32, name="factor")
-        page_words = [reuse.tile([P, HALF], U32, name="page_words0", align_bytes=64, offset=0),
-                      reuse.tile([P, HALF], U32, name="page_words1", align_bytes=64, offset=4 * U)]
-        wa_plane_raw = reuse.tile([P, K], U8, name="wa_plane_raw", offset=4 * U + 4 * HALF - K // 2)
-        f1 = [keep.tile([P, U], F32, name=f"f1_{j}") for j in (0, 1)]
-        f1.append(reuse.tile([P, U], F32, name="f1_2", offset=4 * U + 4 * HALF))
-        f1.append(reuse.tile([P, U], F32, name="f1_3", offset=0))
+        page_words = [keep.tile([P, HALF], U32, name="page_words0", align_bytes=64),
+                      reuse.tile([P, HALF], U32, name="page_words1", align_bytes=64, offset=0)]
+        wa_plane_raw = reuse.tile([P, K], U8, name="wa_plane_raw", offset=4 * HALF - K // 2)
+        wb = reuse.tile([P, K], U32, name="wb", align_bytes=64, offset=4 * HALF)
         wb_plane_raw = keep.tile([P, K], U8, name="wb_plane_raw")
+        f1 = [keep.tile([P, U], F32, name=f"f1_{j}") for j in range(PACK)]
         wb_raw = keep.tile([P, K], I32, name="wb_raw")
         z0a = keep.tile([P, HALF], F32, name="z0a")
         z1a = keep.tile([P, HALF], F32, name="z1a")
@@ -82,8 +80,6 @@ def tile_attend_pagesintonotes_kernel(tc, pages_words, pages_scales, wa_words, w
 
         nc.vector.memset(pool_scales[:].bitcast(I32), 0)
         nc.gpsimd.memset(wa_plane_raw[:].bitcast(I32), 0)
-        nc.vector.memset(wb_plane_raw[:].bitcast(I32), 0)
-        nc.vector.memset(planes[:].bitcast(I32), 0)
 
         pages_rows = pages_words[0].rearrange("p n t -> p (n t)").bitcast(I32)
         nc.sync.dma_start(list_pages[:], offs)
@@ -92,6 +88,8 @@ def tile_attend_pagesintonotes_kernel(tc, pages_words, pages_scales, wa_words, w
         load_scale_rows([nc.sync] * 4, pool_scales, pages_scales)
         nc.sync.dma_start(out=pool_words[:, T // 4:T].bitcast(I32), in_=pages_rows[:, T // 4:T])
         load_scale_rows([nc.sync, nc.sync, nc.sync, nc.gpsimd], wa_plane_raw, wa_scales)
+        nc.gpsimd.memset(wb_plane_raw[:].bitcast(I32), 0)
+        nc.gpsimd.memset(planes[:].bitcast(I32), 0)
         nc.sync.dma_start(out=wb_raw[:], in_=wb_words[0].rearrange("p n t -> p (n t)").bitcast(I32))
         nc.sync.dma_start(list_put[:], offs2)
         load_scale_rows([nc.sync] * 4, wb_plane_raw, wb_scales)
@@ -111,7 +109,8 @@ def tile_attend_pagesintonotes_kernel(tc, pages_words, pages_scales, wa_words, w
         nc.vector.tensor_copy(page_words[1][:], pool_words[:].indirect(list_half(list_pages, 1)))
 
         for j in (1, 0, 2):
-            nc.gpsimd.memset(f1[j][:], 0.0)
+            nc.vector.memset(f1[j][:], 0.0)
+        nc.gpsimd.memset(f1[3][:], 0.0)
         nc.gpsimd.tensor_copy(out=wb[:].bitcast(I32).rearrange("p (j m) -> p j m", j=PACK),
                               in_=wb_raw[:].rearrange("p (m j) -> p j m", j=PACK))
         nc.gpsimd.tensor_copy(out=wb_plane[:].rearrange("p (j m) -> p j m", j=PACK),
@@ -139,7 +138,6 @@ def tile_attend_pagesintonotes_kernel(tc, pages_words, pages_scales, wa_words, w
         nc.vector.tensor_copy(f1[2][:].indirect(list_put[:]), z2[:])
         nc.scalar.activation(places(0, 1), z10b[:, half(1)], COPY)
         nc.scalar.copy(out=z3[:], in_=z_bank(4, [(3, 0), (3, 1)]))
-        nc.gpsimd.memset(f1[3][:], 0.0)
         for h in range(2):
             nc.scalar.activation(places(3, h), z3[:, half(h)], COPY)
 

from contextlib import ExitStack

import concourse.mybir as mybir

D, K, T, U, I, E = 512, 512, 2048, 1024, 512, 256
FLOPS = 2 * D * K * I + 2 * D * K * U + 2 * K * E * I

F32 = mybir.dt.float32
BF16 = mybir.dt.bfloat16
I32 = mybir.dt.int32
U32 = mybir.dt.uint32
U16 = mybir.dt.uint16
U8 = mybir.dt.uint8
FP8X4 = mybir.dt.float8_e4m3fn_x4
FP4X4 = mybir.dt.float4_e2m1fn_x4
COPY = mybir.ActivationFunctionType.Copy
ADD = mybir.AluOpType.add
MULT = mybir.AluOpType.mult

P = 128
PACK = 4
BANK = 512
HALF = I // 2
LIST_COLS = I // 16


def load_scale_rows(queues, plane, scales):
    for r, queue in enumerate(queues):
        queue.dma_start(out=plane[r:P:32, :].bitcast(I32), in_=scales[0][r:16:4, :].bitcast(I32))


def tile_attend_pagesintonotes_kernel(tc, pages_words, pages_scales, wa_words, wa_scales, notes_words, notes_scales,
                                       wb_words, wb_scales, kf, wo_words, wo_scales, offs, offs2, offs3, out):
    nc = tc.nc
    with ExitStack() as ctx:
        keep = ctx.enter_context(tc.tile_pool(name="keep", bufs=1))
        reuse = ctx.enter_context(tc.tile_pool(name="reuse", bufs=1))
        psum = ctx.enter_context(tc.psum_pool(name="psum", bufs=1))

        list_pages = keep.tile([P, LIST_COLS], U16, name="list_pages")
        list_put = keep.tile([P, LIST_COLS], U16, name="list_put")
        list_get = keep.tile([P, LIST_COLS], U16, name="list_get")
        pool_words = keep.tile([P, T], U32, name="pool_words", align_bytes=64)
        pool_scales = keep.tile([P, T], U8, name="pool_scales", align_bytes=64)
        page_scales = keep.tile([P, I], U8, name="page_scales", align_bytes=64)
        wa_raw = keep.tile([P, 2 * K], U8, name="wa_raw")
        notes = keep.tile([P, 2 * U], U8, name="notes", align_bytes=64)
        wo = keep.tile([P, 2 * E], U8, name="wo", align_bytes=64)
        planes = keep.tile([P, U + E], U8, name="planes", align_bytes=64)
        notes_plane = planes[:, 0:U]
        wo_plane = planes[:, U:U + E]
        wa = keep.tile([P, 2 * K], U8, name="wa", align_bytes=64)
        wa_plane = keep.tile([P, K], U8, name="wa_plane", align_bytes=64)
        wb_plane = keep.tile([P, K], U8, name="wb_plane", align_bytes=64)
        factor = keep.tile([P, PACK], F32, name="factor")
        page_words = [keep.tile([P, HALF], U32, name="page_words0", align_bytes=64),
                      reuse.tile([P, HALF], U32, name="page_words1", align_bytes=64, offset=0)]
        wa_plane_raw = reuse.tile([P, K], U8, name="wa_plane_raw", offset=4 * HALF - K // 2)
        wb = reuse.tile([P, K], U32, name="wb", align_bytes=64, offset=4 * HALF)
        wb_plane_raw = keep.tile([P, K], U8, name="wb_plane_raw")
        f1 = [keep.tile([P, U], F32, name=f"f1_{j}") for j in range(PACK)]
        wb_raw = keep.tile([P, K], I32, name="wb_raw")
        z0a = keep.tile([P, HALF], F32, name="z0a")
        z1a = keep.tile([P, HALF], F32, name="z1a")
        z10b = keep.tile([P, I], F32, name="z10b")
        z2 = keep.tile([P, I], F32, name="z2")
        z3 = keep.tile([P, I], F32, name="z3")
        c1 = [keep.tile([P, U], F32, name=f"c1_{j}") for j in range(PACK)]
        picked = [keep.tile([P, PACK, HALF], F32, name=f"picked{h}") for h in range(2)]
        w = [keep.tile([P, HALF, PACK], BF16, name=f"w{h}", align_bytes=64) for h in range(2)]
        w_words = [keep.tile([P, HALF], U32, name=f"w_words{h}", align_bytes=64) for h in range(2)]
        w_plane = [keep.tile([P, HALF], U8, name=f"w_plane{h}", align_bytes=64) for h in range(2)]
        result = [[keep.tile([P, HALF], F32, name=f"result{h}{t}") for t in range(2)] for h in range(2)]

        def half(h):
            return slice(HALF * h, HALF * (h + 1))

        def list_half(listed, h):
            return listed[:, LIST_COLS // 2 * h:LIST_COLS // 2 * (h + 1)]

        nc.vector.memset(pool_scales[:].bitcast(I32), 0)
        nc.gpsimd.memset(wa_plane_raw[:].bitcast(I32), 0)

        pages_rows = pages_words[0].rearrange("p n t -> p (n t)").bitcast(I32)
        nc.sync.dma_start(list_pages[:], offs)
        nc.sync.dma_start(out=wa_raw[:].bitcast(I32), in_=wa_words[0].bitcast(I32))
        nc.sync.dma_start(out=pool_words[:, 0:T // 4].bitcast(I32), in_=pages_rows[:, 0:T // 4])
        load_scale_rows([nc.sync] * 4, pool_scales, pages_scales)
        nc.sync.dma_start(out=pool_words[:, T // 4:T].bitcast(I32), in_=pages_rows[:, T // 4:T])
        load_scale_rows([nc.sync, nc.sync, nc.sync, nc.gpsimd], wa_plane_raw, wa_scales)
        nc.gpsimd.memset(wb_plane_raw[:].bitcast(I32), 0)
        nc.gpsimd.memset(planes[:].bitcast(I32), 0)
        nc.sync.dma_start(out=wb_raw[:], in_=wb_words[0].rearrange("p n t -> p (n t)").bitcast(I32))
        nc.sync.dma_start(list_put[:], offs2)
        load_scale_rows([nc.sync] * 4, wb_plane_raw, wb_scales)
        nc.sync.dma_start(out=notes[:].bitcast(I32), in_=notes_words[0].bitcast(I32))
        load_scale_rows([nc.sync] * 4, notes_plane, notes_scales)
        nc.sync.dma_start(list_get[:], offs3)
        nc.sync.dma_start(out=factor[:], in_=kf.rearrange("(p j) o -> p (j o)", j=PACK))
        nc.sync.dma_start(out=wo[:].bitcast(I32), in_=wo_words[0].bitcast(I32))
        load_scale_rows([nc.sync] * 4, wo_plane, wo_scales)

        nc.vector.tensor_copy(page_scales[:], pool_scales[:].indirect(list_pages[:]))
        nc.scalar.copy(out=wa[:].bitcast(U16).rearrange("p (j m) -> p j m", j=PACK),
                       in_=wa_raw[:].bitcast(U16).rearrange("p (m j) -> p j m", j=PACK))
        nc.vector.tensor_copy(page_words[0][:], pool_words[:].indirect(list_half(list_pages, 0)))
        nc.vector.tensor_copy(out=wa_plane[:].rearrange("p (j m) -> p j m", j=PACK),
                              in_=wa_plane_raw[:].rearrange("p (m j) -> p j m", j=PACK))
        nc.vector.tensor_copy(page_words[1][:], pool_words[:].indirect(list_half(list_pages, 1)))

        for j in (1, 0, 2):
            nc.vector.memset(f1[j][:], 0.0)
        nc.gpsimd.memset(f1[3][:], 0.0)
        nc.gpsimd.tensor_copy(out=wb[:].bitcast(I32).rearrange("p (j m) -> p j m", j=PACK),
                              in_=wb_raw[:].rearrange("p (m j) -> p j m", j=PACK))
        nc.gpsimd.tensor_copy(out=wb_plane[:].rearrange("p (j m) -> p j m", j=PACK),
                              in_=wb_plane_raw[:].rearrange("p (m j) -> p j m", j=PACK))

        def z_bank(number, parts):
            bank = psum.tile([P, BANK], F32, name=f"z_bank{number}", tag=f"bank{number}")
            for place, (j, h) in enumerate(parts):
                nc.tensor.matmul_mx(out=bank[:, half(place)], lhsT=wa[:, 2 * P * j:2 * P * (j + 1)].bitcast(FP4X4),
                                    lhsT_scale=wa_plane[:, P * j:P * (j + 1)],
                                    rhs=page_words[h][:].bitcast(FP8X4), rhs_scale=page_scales[:, half(h)],
                                    start=True, stop=True)
            return bank[:, 0:HALF * len(parts)]

        def places(j, h):
            return f1[j][:].indirect(list_half(list_put, h))

        nc.scalar.activation(z1a[:], z_bank(0, [(1, 0)]), COPY)
        nc.vector.tensor_copy(out=z0a[:], in_=z_bank(1, [(0, 0)]))
        nc.scalar.activation(places(1, 0), z1a[:], COPY)
        nc.vector.tensor_copy(places(0, 0), z0a[:])
        nc.scalar.copy(out=z10b[:], in_=z_bank(2, [(1, 1), (0, 1)]))
        nc.vector.tensor_copy(out=z2[:], in_=z_bank(3, [(2, 0), (2, 1)]))
        nc.scalar.activation(places(1, 1), z10b[:, half(0)], COPY)
        nc.vector.tensor_copy(f1[2][:].indirect(list_put[:]), z2[:])
        nc.scalar.activation(places(0, 1), z10b[:, half(1)], COPY)
        nc.scalar.copy(out=z3[:], in_=z_bank(4, [(3, 0), (3, 1)]))
        for h in range(2):
            nc.scalar.activation(places(3, h), z3[:, half(h)], COPY)

        def look_up(j, h):
            return c1[j][:].indirect(list_half(list_get, h))

        for n, j in enumerate((1, 2, 0, 3)):
            if j == 3:
                nc.vector.tensor_copy(picked[0][:, 2, :], look_up(2, 0))
                nc.vector.tensor_copy(picked[0][:, 0, :], look_up(0, 0))
            for u in range(U // BANK):
                bank = psum.tile([P, BANK], F32, name=f"h_bank{j}{u}", tag=f"bank{(5 + 2 * n + u) % 8}")
                nc.tensor.matmul_mx(out=bank[:], lhsT=wb[:, P * j:P * (j + 1)].bitcast(FP8X4),
                                    lhsT_scale=wb_plane[:, P * j:P * (j + 1)],
                                    rhs=notes[:, 2 * BANK * u:2 * BANK * (u + 1)].bitcast(FP4X4),
                                    rhs_scale=notes_plane[:, BANK * u:BANK * (u + 1)], start=True, stop=True)
                nc.vector.tensor_tensor(out=c1[j][:, BANK * u:BANK * (u + 1)], in0=bank[:],
                                        in1=f1[j][:, BANK * u:BANK * (u + 1)], op=ADD)
        nc.vector.tensor_copy(picked[0][:, 3, :], look_up(3, 0))
        for j, h in ((1, 0), (1, 1), (2, 1), (0, 1), (3, 1)):
            nc.scalar.activation(picked[h][:, j, :], look_up(j, h), COPY)

        spread = factor[:].rearrange("p (c j i) -> p c j i", c=1, i=1).to_broadcast([P, HALF // 2, PACK, 2])
        for h in range(2):
            nc.vector.tensor_tensor(out=w[h][:].rearrange("p (c i) j -> p c j i", i=2),
                                    in0=picked[h][:].rearrange("p j (c i) -> p c j i", i=2), in1=spread, op=MULT)
            nc.vector.quantize_mx(out=w_words[h][:].bitcast(FP8X4), scales=w_plane[h][:],
                                  in_=w[h][:].rearrange("p i j -> p (i j)"))
            for t in range(E // P):
                bank = psum.tile([P, BANK], F32, name=f"y_bank{h}{t}", tag=f"bank{(5 + 2 * h + t) % 8}")
                nc.tensor.matmul_mx(out=bank[:, 0:HALF], lhsT=wo[:, 2 * P * t:2 * P * (t + 1)].bitcast(FP4X4),
                                    lhsT_scale=wo_plane[:, P * t:P * (t + 1)],
                                    rhs=w_words[h][:].bitcast(FP8X4), rhs_scale=w_plane[h][:], start=True, stop=True)
                if (h, t) == (1, 1):
                    nc.vector.tensor_copy(out=result[h][t][:], in_=bank[:, 0:HALF])
                else:
                    nc.scalar.copy(out=result[h][t][:], in_=bank[:, 0:HALF])
                nc.sync.dma_start(out=out[P * t:P * (t + 1), half(h)], in_=result[h][t][:])
